import numpy as np
import ml_dtypes


def mxq(x, axis, fmt="e4m3"):
    dtype, down = {"e4m3": (ml_dtypes.float8_e4m3fn, 7), "e5m2": (ml_dtypes.float8_e5m2, 14)}[fmt]
    v = np.moveaxis(np.asarray(x, np.float32).astype(ml_dtypes.bfloat16).astype(np.float64), axis, -1)
    blocks = v.reshape(v.shape[:-1] + (-1, 32))
    amax = np.abs(blocks).max(-1, keepdims=True)
    byte = np.maximum(np.where(amax > 0, np.frexp(amax)[1] - 1 + 127, 0) - down, 1)
    scale = np.exp2(byte - 127.0)
    codes = (blocks / scale).astype(np.float32).astype(dtype).astype(np.float64)
    return np.moveaxis((codes * scale).reshape(v.shape), -1, axis)


WIDE = False


def mx_kscale(k):
    if not WIDE:
        return np.ones(k)
    levels = np.array([10, -10, 5, -5, 0])
    if k % 512:
        return np.exp2(np.random.permutation(np.resize(levels, k // 32))).repeat(32)
    a = np.empty((k // 512, 16))
    for p in range(k // 512):
        a[p, :8] = np.random.permutation(np.resize(levels, 8))
        for g in range(8):
            far = levels[np.abs(levels - a[p, g]) >= 10]
            a[p, g + 8] = far[np.random.randint(len(far))]
    return np.exp2(a.ravel()).repeat(32)


BF16 = ml_dtypes.bfloat16


def bf(x):
    return np.asarray(x, np.float32).astype(BF16)


def f64(x):
    return np.asarray(x).astype(np.float64)

E4M3FN = np.array([(-1.0 if i & 128 else 1.0) * ((1.0 + (i & 7) / 8.0) * 2.0 ** (((i >> 3) & 15) - 7) if i & 120 else (i & 7) * 2.0 ** -9) for i in range(256)])


def e4m3fn_bytes(y):
    return np.clip(np.asarray(y, np.float64), -448.0, 448.0).astype(np.float32).astype(ml_dtypes.float8_e4m3fn).view(np.uint8)


def e4m3fn_values(b):
    return E4M3FN[b]

def planes(Y):
    n, m = Y.shape
    b = f64(bf(Y)).reshape(n // 32, 32, m)
    amax = np.abs(b).max(1)
    byte = np.clip(np.where(amax > 0, np.frexp(amax)[1] - 1 + 127 - 7, 1), 1, 254)
    codes = (b * np.exp2(127.0 - byte)[:, None, :]).reshape(n, m).astype(np.float32).astype(ml_dtypes.float8_e4m3fn).view(np.uint8)
    words = codes.reshape(n // 512, 128, 4, m).transpose(0, 1, 3, 2)
    return np.ascontiguousarray(words), np.ascontiguousarray(byte.astype(np.uint8).reshape(n // 512, 16, m))


T, K, A, B = 1024, 2048, 1536, 128

BIAS_SIZE = 0.3
RANGE_SPREAD = 0.8
CODE_MAX = 448.0


def setup_inputs():
    s = mx_kscale(K)
    X = np.random.randn(T, K) * s[None, :]
    block_max = np.abs(X).reshape(T, K // B, B).max(axis=2)
    X_scale = (block_max / CODE_MAX).astype(np.float32)
    X_bytes = e4m3fn_bytes(X / np.repeat(f64(X_scale), B, axis=1))
    W = np.random.randn(K, A) / np.sqrt(K) / s[:, None]
    bias = BIAS_SIZE * np.random.randn(A)
    half_range = np.exp(RANGE_SPREAD * np.random.randn(A))
    return {
        "X_bytes": X_bytes,
        "X_scale": X_scale,
        "W": bf(W),
        "bias": bf(bias),
        "half_range": bf(half_range),
    }


def reference(X_bytes, X_scale, W, bias, half_range):
    X = e4m3fn_values(X_bytes) * np.repeat(f64(X_scale), B, axis=1)
    z = mxq(X, 1, "e4m3") @ mxq(f64(W), 0, "e4m3")
    u = np.tanh(z + f64(bias))
    y = u * f64(half_range)
    words, scales = planes(y.T)
    return y, words, scales

@@ -1,0 +1,279 @@
+from contextlib import ExitStack
+
+import concourse.mybir as mybir
+from concourse.masks import make_identity
+
+T, K, A = 1024, 2048, 1536
+FLOPS = 2 * T * K * A
+
+F32 = mybir.dt.float32
+BF16 = mybir.dt.bfloat16
+I32 = mybir.dt.int32
+U32 = mybir.dt.uint32
+U8 = mybir.dt.uint8
+FP8 = mybir.dt.float8_e4m3fn
+FP8X4 = mybir.dt.float8_e4m3fn_x4
+MULT = mybir.AluOpType.mult
+COPY = mybir.ActivationFunctionType.Copy
+TANH = mybir.ActivationFunctionType.Tanh
+
+P = 128
+PACK = 4
+SPAN = P * PACK
+PASSES = K // SPAN
+GROUPS = A // SPAN
+HALVES = T // SPAN
+ROWS = SPAN // P
+BLOCK = 128
+CUT = ((40, 16, 16, 24), (32, 40, 40, 40), (32, 48, 64, 64))
+SS = ()
+VS = ((2, 1, 1), (2, 1, 3))
+
+
+def tile_tanh_policy_action_head_b1_kernel(tc, X_bytes, X_scale, W, bias, half_range, out_0, out_1, out_2):
+    nc = tc.nc
+    with ExitStack() as ctx:
+        keep = ctx.enter_context(tc.tile_pool(name="keep", bufs=1))
+        flow = ctx.enter_context(tc.tile_pool(name="flow", bufs=3))
+        psum = ctx.enter_context(tc.psum_pool(name="psum", bufs=1))
+
+        x_raw, x_sc, w_raw, x_wide, x_in, w_in = {}, {}, {}, {}, {}, {}
+        x_codes, x_scales, w_codes, w_scales = {}, {}, {}, {}
+        acc, y_t, y_in, y_scales, turned = {}, {}, {}, {}, {}
+
+        def load_x_scale(h):
+            x_sc[h] = keep.tile([P, ROWS, K // BLOCK], F32, name="x_sc%d" % h)
+            nc.sync.dma_start(out=x_sc[h][:], in_=X_scale[SPAN * h : SPAN * (h + 1), :].rearrange("(r p) j -> p r j", p=P))
+
+        def load_x(h, c):
+            x_raw[h, c] = keep.tile([P, ROWS, SPAN], U8, name="x_raw%d%d" % (h, c))
+            src = X_bytes[SPAN * h : SPAN * (h + 1), SPAN * c : SPAN * (c + 1)]
+            nc.sync.dma_start(out=x_raw[h, c][:], in_=src.rearrange("(r p) k -> p r k", p=P))
+
+        def load_w(g, c):
+            w_raw[g, c] = keep.tile([P, PACK, SPAN], BF16, name="w_raw%d%d" % (g, c))
+            src = W[SPAN * c : SPAN * (c + 1), SPAN * g : SPAN * (g + 1)]
+            nc.sync.dma_start(out=w_raw[g, c][:], in_=src.rearrange("(p j) a -> p j a", j=PACK))
+
+        def widen(h, c, r):
+            x_wide[h, c, r] = flow.tile([P, SPAN], BF16, name="x_wide", bufs=8)
+            sorted_view = x_wide[h, c, r][:].rearrange("p (u w e) -> p w u e", u=2, e=2)
+            for q in range(SPAN // BLOCK):
+                j = c * (SPAN // BLOCK) + q
+                nc.vector.tensor_scalar(
+                    out=sorted_view[:, 32 * q : 32 * (q + 1)],
+                    in0=x_raw[h, c][:, r, BLOCK * q : BLOCK * (q + 1)].bitcast(FP8).rearrange("p (w u e) -> p w u e", u=2, e=2),
+                    scalar1=x_sc[h][:, r, j : j + 1],
+                    scalar2=None,
+                    op0=MULT,
+                )
+
+        def turn_x(h, c, b, bank):
+            turned[h, c, b] = psum.tile([P, 2, 2, P], F32, name="bank%d" % bank)
+            for i in range(2):
+                words = x_wide[h, c, 2 * b + i][:].bitcast(F32)
+                for u in range(2):
+                    nc.tensor.transpose(turned[h, c, b][:, i, u, :], words[:, P * u : P * (u + 1)], ident[:])
+
+        def spill_x(h, c, b):
+            if b == 0:
+                x_in[h, c] = flow.tile([P, SPAN * PACK], BF16, name="x_in", align_bytes=64)
+            dst = x_in[h, c][:].bitcast(F32)[:, 4 * P * b : 4 * P * (b + 1)]
+            nc.scalar.copy(
+                out=dst.rearrange("p (i m u) -> p i m u", i=2, u=2),
+                in_=turned[h, c, b][:].rearrange("p i u m -> p i m u"),
+            )
+
+        def quant_x(h, c):
+            x_codes[h, c] = keep.tile([P, SPAN], U32, name="x_codes%d%d" % (h, c), align_bytes=64)
+            x_scales[h, c] = keep.tile([P, SPAN], U8, name="x_scales%d%d" % (h, c), align_bytes=64)
+            nc.vector.quantize_mx(out=x_codes[h, c][:].bitcast(FP8X4), scales=x_scales[h, c][:], in_=x_in[h, c][:])
+
+        def weave_w(g, c, engine, lo, hi):
+            if lo >= hi:
+                return
+            if (g, c) not in w_in:
+                w_in[g, c] = flow.tile([P, SPAN * PACK], BF16, name="w_in", bufs=4, align_bytes=64)
+            dst = w_in[g, c][:].rearrange("p (t n i j) -> p n t i j", t=PACK, i=2, j=PACK)
+            src = w_raw[g, c][:].rearrange("p j (n i t) -> p n t i j", i=2, t=PACK)
+            if engine == "vector":
+                nc.vector.tensor_copy(out=dst[:, lo:hi], in_=src[:, lo:hi])
+            else:
+                nc.scalar.copy(out=dst[:, lo:hi], in_=src[:, lo:hi])
+
+        def quant_w(g, c):
+            w_codes[g, c] = keep.tile([P, SPAN], U32, name="w_codes%d%d" % (g, c), align_bytes=64)
+            w_scales[g, c] = keep.tile([P, SPAN], U8, name="w_scales%d%d" % (g, c), align_bytes=64)
+            nc.vector.quantize_mx(out=w_codes[g, c][:].bitcast(FP8X4), scales=w_scales[g, c][:], in_=w_in[g, c][:])
+
+        def mm(g, h, t, c, bank):
+            if c == 0:
+                acc[g, h, t] = psum.tile([P, SPAN], F32, name="bank%d" % bank)
+            cols = slice(P * t, P * (t + 1))
+            nc.tensor.matmul_mx(
+                out=acc[g, h, t][:],
+                lhsT=w_codes[g, c][:, cols].bitcast(FP8X4),
+                lhsT_scale=w_scales[g, c][:, cols],
+                rhs=x_codes[h, c][:].bitcast(FP8X4),
+                rhs_scale=x_scales[h, c][:],
+                start=(c == 0),
+                stop=(c == PASSES - 1),
+            )
+
+        def mm_pass(g, h, c, bank0, slots=range(PACK)):
+            for t in slots:
+                mm(g, h, t, c, bank0 + t)
+
+        def mm_slot(g, h, t, bank):
+            for c in range(PASSES):
+                mm(g, h, t, c, bank)
+
+        def squash(g, h, t):
+            if t == 0:
+                y_t[g, h] = keep.tile([P, PACK, SPAN], F32, name="y_t%d%d" % (g, h))
+            col = PACK * g + t
+            nc.scalar.activation(out=y_t[g, h][:, t, :], in_=acc[g, h, t][:], func=TANH, bias=vecs[:, 0, col : col + 1])
+
+        def stretch(g, h, t, on_vector=True):
+            col = PACK * g + t
+            row = y_t[g, h][:, t, :]
+            if on_vector:
+                nc.vector.tensor_scalar(out=row, in0=row, scalar1=vecs[:, 1, col : col + 1], scalar2=None, op0=MULT)
+            else:
+                nc.scalar.activation(out=row, in_=row, func=COPY, scale=vecs[:, 1, col : col + 1])
+
+        def turn_y(g, h, r, bank):
+            turned[g, h, r, "y"] = psum.tile([P, PACK, P], F32, name="bank%d" % bank)
+            for t in range(PACK):
+                nc.tensor.transpose(turned[g, h, r, "y"][:, t, :], y_t[g, h][:, t, P * r : P * (r + 1)], ident[:])
+
+        def spill_y(g, h, r, on_vector=False):
+            y_out = flow.tile([P, SPAN], F32, name="y_out", bufs=6)
+            dst = y_out[:].rearrange("p (m t) -> p m t", t=PACK)
+            src = turned[g, h, r, "y"][:].rearrange("p t m -> p m t")
+            if on_vector:
+                nc.vector.tensor_copy(out=dst, in_=src)
+            else:
+                nc.scalar.copy(out=dst, in_=src)
+            m0 = SPAN * h + P * r
+            nc.sync.dma_start(out=out_0[m0 : m0 + P, SPAN * g : SPAN * (g + 1)], in_=y_out[:])
+
+        def weave_y(g, h):
+            y_in[g, h] = flow.tile([P, SPAN * PACK], BF16, name="y_in", bufs=2, align_bytes=64)
+            nc.vector.tensor_copy(
+                out=y_in[g, h][:].rearrange("p (n i t) -> p n t i", i=4, t=PACK),
+                in_=y_t[g, h][:].rearrange("p t (n i) -> p n t i", i=4),
+            )
+
+        def quant_y(g, h):
+            if h == 0:
+                y_scales[g] = keep.tile([P, T], U8, name="y_scales%d" % g, align_bytes=64)
+            y_words = flow.tile([P, SPAN], U32, name="y_words", align_bytes=64)
+            cols = slice(SPAN * h, SPAN * (h + 1))
+            nc.vector.quantize_mx(out=y_words[:].bitcast(FP8X4), scales=y_scales[g][:, cols], in_=y_in[g, h][:])
+            nc.sync.dma_start(out=out_1[g, :, cols, :].rearrange("p m t -> p (m t)").bitcast(I32), in_=y_words[:].bitcast(I32))
+            if h == HALVES - 1:
+                for q in range(4):
+                    nc.sync.dma_start(out=out_2[g, 4 * q : 4 * q + 4, :].bitcast(I32), in_=y_scales[g][32 * q : 32 * q + 4, :].bitcast(I32))
+
+        load_x_scale(0)
+        for c in range(PASSES):
+            load_x(0, c)
+            load_w(0, c)
+        vecs_raw = keep.tile([P, 2, 16], BF16, name="vecs_raw")
+        for i, vec in enumerate((bias, half_range)):
+            nc.sync.dma_start(
+                out=vecs_raw[:, i, : GROUPS * PACK].rearrange("p (g t) -> p g t", t=PACK),
+                in_=vec.rearrange("(g p t) -> p g t", p=P, t=PACK),
+            )
+        load_x_scale(1)
+        for c in range(PASSES):
+            load_w(1, c)
+        for c in range(PASSES):
+            load_x(1, c)
+        for c in range(PASSES):
+            load_w(2, c)
+
+        ident = keep.tile([P, P], F32, name="ident")
+        make_identity(nc, ident[:])
+        warm = keep.tile([P, 1], F32, name="warm")
+        nc.vector.memset(warm[:], 0.0)
+        nc.scalar.activation(out=warm[:], in_=warm[:], func=TANH)
+        vecs = keep.tile([P, 2, GROUPS * PACK], F32, name="vecs")
+
+
+        V, S = "vector", "scalar"
+        N = 64
+
+        def x_chunk(h, c, bank):
+            for b in range(2):
+                widen(h, c, 2 * b)
+                widen(h, c, 2 * b + 1)
+                turn_x(h, c, b, bank + b)
+            for b in range(2):
+                spill_x(h, c, b)
+            quant_x(h, c)
+
+        def w_chunk(g, c):
+            cut = CUT[g][c]
+            weave_w(g, c, V, 0, cut)
+            mid = (cut + N) // 2 if N - cut > 32 else N
+            weave_w(g, c, S, cut, mid)
+            weave_w(g, c, S, mid, N)
+            quant_w(g, c)
+
+        def act(g, h):
+            for t in range(PACK):
+                squash(g, h, t)
+                stretch(g, h, t, (g, h, t) not in SS)
+
+        def out(g, h, bank):
+            for r in range(ROWS):
+                turn_y(g, h, r, bank + r)
+                spill_y(g, h, r, (g, h, r) in VS)
+
+        def planes(g, h):
+            weave_y(g, h)
+            quant_y(g, h)
+
+        x_chunk(0, 0, 4)
+        for c in range(PASSES):
+            if c + 1 < PASSES:
+                x_chunk(0, c + 1, 4 + 2 * ((c + 1) % 2))
+            w_chunk(0, c)
+            mm_pass(0, 0, c, 0)
+        nc.vector.tensor_copy(out=vecs[:], in_=vecs_raw[:, :, : GROUPS * PACK])
+        for c in range(PASSES):
+            w_chunk(1, c)
+            mm_pass(1, 0, c, 4)
+            if c == 0:
+                act(0, 0)
+        out(0, 0, 0)
+        for c in range(PASSES):
+            x_chunk(1, c, 2 * (c % 2))
+            if c == 0:
+                act(1, 0)
+            mm_pass(0, 1, c, 4)
+        for c in range(PASSES):
+            w_chunk(2, c)
+        act(0, 1)
+        for t in range(PACK):
+            mm_slot(1, 1, t, 4 + t)
+        out(1, 0, 0)
+        act(1, 1)
+        for t in range(PACK):
+            mm_slot(2, 0, t, 4 + t)
+        out(0, 1, 0)
+        act(2, 0)
+        out(1, 1, 0)
+        for t in range(PACK):
+            mm_slot(2, 1, t, 4 + t)
+        out(2, 0, 0)
+        act(2, 1)
+        planes(0, 0)
+        planes(1, 0)
+        planes(0, 1)
+        planes(1, 1)
+        planes(2, 0)
+        out(2, 1, 4)
+        planes(2, 1)

@@ -25,9 +25,7 @@ GROUPS = A // SPAN
 HALVES = T // SPAN
 ROWS = SPAN // P
 BLOCK = 128
-CUT = ((40, 16, 16, 24), (32, 40, 40, 40), (32, 48, 64, 64))
-SS = ()
-VS = ((2, 1, 1), (2, 1, 3))
+CUT = ((32, 16, 24, 40), (24, 48, 40, 40), (40, 64, 64, 48))
 
 
 def tile_tanh_policy_action_head_b1_kernel(tc, X_bytes, X_scale, W, bias, half_range, out_0, out_1, out_2):
@@ -36,6 +34,7 @@ def tile_tanh_policy_action_head_b1_kernel(tc, X_bytes, X_scale, W, bias, half_r
         keep = ctx.enter_context(tc.tile_pool(name="keep", bufs=1))
         flow = ctx.enter_context(tc.tile_pool(name="flow", bufs=3))
         psum = ctx.enter_context(tc.psum_pool(name="psum", bufs=1))
+        ctx.enter_context(tc.manual_schedule())
 
         x_raw, x_sc, w_raw, x_wide, x_in, w_in = {}, {}, {}, {}, {}, {}
         x_codes, x_scales, w_codes, w_scales = {}, {}, {}, {}
@@ -129,7 +128,7 @@ def tile_tanh_policy_action_head_b1_kernel(tc, X_bytes, X_scale, W, bias, half_r
                 mm(g, h, t, c, bank)
 
         def squash(g, h, t):
-            if t == 0:
+            if (g, h) not in y_t:
                 y_t[g, h] = keep.tile([P, PACK, SPAN], F32, name="y_t%d%d" % (g, h))
             col = PACK * g + t
             nc.scalar.activation(out=y_t[g, h][:, t, :], in_=acc[g, h, t][:], func=TANH, bias=vecs[:, 0, col : col + 1])
@@ -148,7 +147,7 @@ def tile_tanh_policy_action_head_b1_kernel(tc, X_bytes, X_scale, W, bias, half_r
                 nc.tensor.transpose(turned[g, h, r, "y"][:, t, :], y_t[g, h][:, t, P * r : P * (r + 1)], ident[:])
 
         def spill_y(g, h, r, on_vector=False):
-            y_out = flow.tile([P, SPAN], F32, name="y_out", bufs=6)
+            y_out = flow.tile([P, SPAN], F32, name="y_out", bufs=8)
             dst = y_out[:].rearrange("p (m t) -> p m t", t=PACK)
             src = turned[g, h, r, "y"][:].rearrange("p t m -> p m t")
             if on_vector:
@@ -177,8 +176,10 @@ def tile_tanh_policy_action_head_b1_kernel(tc, X_bytes, X_scale, W, bias, half_r
                     nc.sync.dma_start(out=out_2[g, 4 * q : 4 * q + 4, :].bitcast(I32), in_=y_scales[g][32 * q : 32 * q + 4, :].bitcast(I32))
 
         load_x_scale(0)
+        load_x(0, 0)
         for c in range(PASSES):
-            load_x(0, c)
+            if c + 1 < PASSES:
+                load_x(0, c + 1)
             load_w(0, c)
         vecs_raw = keep.tile([P, 2, 16], BF16, name="vecs_raw")
         for i, vec in enumerate((bias, half_range)):
@@ -205,75 +206,182 @@ def tile_tanh_policy_action_head_b1_kernel(tc, X_bytes, X_scale, W, bias, half_r
         V, S = "vector", "scalar"
         N = 64
 
-        def x_chunk(h, c, bank):
-            for b in range(2):
-                widen(h, c, 2 * b)
-                widen(h, c, 2 * b + 1)
-                turn_x(h, c, b, bank + b)
-            for b in range(2):
-                spill_x(h, c, b)
-            quant_x(h, c)
+        def x_half(h, c, b, bank0):
+            widen(h, c, 2 * b)
+            widen(h, c, 2 * b + 1)
+            turn_x(h, c, b, bank0 + 2 * (c % 2) + b)
 
-        def w_chunk(g, c):
-            cut = CUT[g][c]
-            weave_w(g, c, V, 0, cut)
-            mid = (cut + N) // 2 if N - cut > 32 else N
-            weave_w(g, c, S, cut, mid)
-            weave_w(g, c, S, mid, N)
-            quant_w(g, c)
+        def wv(g, c):
+            weave_w(g, c, V, 0, CUT[g][c])
 
-        def act(g, h):
-            for t in range(PACK):
-                squash(g, h, t)
-                stretch(g, h, t, (g, h, t) not in SS)
+        def ws(g, c):
+            weave_w(g, c, S, CUT[g][c], N)
 
-        def out(g, h, bank):
-            for r in range(ROWS):
-                turn_y(g, h, r, bank + r)
-                spill_y(g, h, r, (g, h, r) in VS)
-
-        def planes(g, h):
-            weave_y(g, h)
-            quant_y(g, h)
-
-        x_chunk(0, 0, 4)
+        x_half(0, 0, 0, 4)
+        x_half(0, 0, 1, 4)
+        spill_x(0, 0, 0)
+        spill_x(0, 0, 1)
+        x_half(0, 1, 0, 4)
+        x_half(0, 1, 1, 4)
         for c in range(PASSES):
+            ws(0, c)
+            if c == 3:
+                quant_w(0, 2)
+                mm_pass(0, 0, 2, 0)
+            wv(0, c)
+            quant_x(0, c)
             if c + 1 < PASSES:
-                x_chunk(0, c + 1, 4 + 2 * ((c + 1) % 2))
-            w_chunk(0, c)
-            mm_pass(0, 0, c, 0)
+                spill_x(0, c + 1, 0)
+                spill_x(0, c + 1, 1)
+            if c + 2 < PASSES:
+                x_half(0, c + 2, 0, 4)
+                quant_w(0, c)
+                mm_pass(0, 0, c, 0, (0, 1))
+                x_half(0, c + 2, 1, 4)
+                mm_pass(0, 0, c, 0, (2, 3))
+        ws(1, 0)
+        wv(1, 0)
+        quant_w(0, 3)
+        mm_pass(0, 0, 3, 0)
         nc.vector.tensor_copy(out=vecs[:], in_=vecs_raw[:, :, : GROUPS * PACK])
-        for c in range(PASSES):
-            w_chunk(1, c)
-            mm_pass(1, 0, c, 4)
-            if c == 0:
-                act(0, 0)
-        out(0, 0, 0)
-        for c in range(PASSES):
-            x_chunk(1, c, 2 * (c % 2))
-            if c == 0:
-                act(1, 0)
-            mm_pass(0, 1, c, 4)
-        for c in range(PASSES):
-            w_chunk(2, c)
-        act(0, 1)
+        def x1(c, b):
+            widen(1, c, 2 * b)
+            widen(1, c, 2 * b + 1)
+
+        wv(1, 1)
+        ws(1, 1)
+        quant_w(1, 0)
+        mm_pass(1, 0, 0, 4)
+        wv(1, 2)
+        ws(1, 2)
+        squash(0, 0, 2)
+        squash(0, 0, 3)
+        quant_w(1, 1)
+        mm_pass(1, 0, 1, 4)
+        x1(0, 0)
+        turn_x(1, 0, 0, 2)
+        wv(1, 3)
+        ws(1, 3)
+        squash(0, 0, 0)
+        squash(0, 0, 1)
+        quant_w(1, 2)
+        mm_pass(1, 0, 2, 4)
+        x1(0, 1)
+        turn_x(1, 0, 1, 3)
+        quant_w(1, 3)
+        mm_pass(1, 0, 3, 4)
+        spill_x(1, 0, 0)
+        spill_x(1, 0, 1)
+        x1(1, 0)
+        turn_x(1, 1, 0, 0)
+        x1(1, 1)
+        turn_x(1, 1, 1, 1)
         for t in range(PACK):
+            squash(1, 0, t)
+        quant_x(1, 0)
+        spill_x(1, 1, 0)
+        spill_x(1, 1, 1)
+        x1(2, 0)
+        turn_x(1, 2, 0, 2)
+        mm_pass(0, 1, 0, 4, (0, 1))
+        x1(2, 1)
+        turn_x(1, 2, 1, 3)
+        mm_pass(0, 1, 0, 4, (2, 3))
+        for t in range(PACK):
+            stretch(0, 0, t)
+        quant_x(1, 1)
+        spill_x(1, 2, 0)
+        spill_x(1, 2, 1)
+        x1(3, 0)
+        turn_x(1, 3, 0, 0)
+        mm_pass(0, 1, 1, 4, (0, 1))
+        x1(3, 1)
+        turn_x(1, 3, 1, 1)
+        mm_pass(0, 1, 1, 4, (2, 3))
+        turn_y(0, 0, 0, 2)
+        turn_y(0, 0, 1, 3)
+        wv(2, 0)
+        ws(2, 0)
+        quant_x(1, 2)
+        mm_pass(0, 1, 2, 4)
+        spill_x(1, 3, 0)
+        spill_x(1, 3, 1)
+        turn_y(0, 0, 2, 0)
+        turn_y(0, 0, 3, 1)
+        wv(2, 1)
+        ws(2, 1)
+        quant_x(1, 3)
+        mm_pass(0, 1, 3, 4)
+        for r in range(ROWS):
+            spill_y(0, 0, r)
+        quant_w(2, 0)
+        for t in range(PACK):
+            stretch(1, 0, t)
+        for r in range(ROWS):
+            turn_y(1, 0, r, (r + 2) % 4)
+        wv(2, 2)
+        ws(2, 2)
+        quant_w(2, 1)
+        for t in range(PACK):
+            squash(0, 1, t)
             mm_slot(1, 1, t, 4 + t)
-        out(1, 0, 0)
-        act(1, 1)
+        wv(2, 3)
+        ws(2, 3)
+        quant_w(2, 2)
+        stretch(0, 1, 0)
+        quant_w(2, 3)
+        for t in range(1, PACK):
+            stretch(0, 1, t)
+        weave_y(0, 0)
         for t in range(PACK):
+            squash(1, 1, t)
+            spill_y(1, 0, t)
             mm_slot(2, 0, t, 4 + t)
-        out(0, 1, 0)
-        act(2, 0)
-        out(1, 1, 0)
+        for r in range(ROWS):
+            turn_y(0, 1, r, r)
+        stretch(1, 1, 0)
+        quant_y(0, 0)
+        weave_y(1, 0)
+        for t in range(1, PACK):
+            stretch(1, 1, t)
+        quant_y(1, 0)
+        weave_y(0, 1)
         for t in range(PACK):
-            mm_slot(2, 1, t, 4 + t)
-        out(2, 0, 0)
-        act(2, 1)
-        planes(0, 0)
-        planes(1, 0)
-        planes(0, 1)
-        planes(1, 1)
-        planes(2, 0)
-        out(2, 1, 4)
-        planes(2, 1)
+            squash(2, 0, t)
+        for r in range(ROWS):
+            spill_y(0, 1, r)
+        mm_slot(2, 1, 0, 4)
+        mm_slot(2, 1, 1, 5)
+        for r in range(ROWS):
+            turn_y(1, 1, r, r)
+        mm_slot(2, 1, 2, 6)
+        mm_slot(2, 1, 3, 7)
+        stretch(2, 0, 0)
+        quant_y(0, 1)
+        weave_y(1, 1)
+        for t in range(1, PACK):
+            stretch(2, 0, t)
+        quant_y(1, 1)
+        weave_y(2, 0)
+        squash(2, 1, 0)
+        squash(2, 1, 1)
+        for r in range(ROWS):
+            spill_y(1, 1, r)
+            if r in (1, 2):
+                squash(2, 1, r + 1)
+        for r in range(ROWS):
+            turn_y(2, 0, r, r)
+        stretch(2, 1, 0)
+        quant_y(2, 0)
+        for t in range(1, PACK):
+            stretch(2, 1, t)
+        for r in range(ROWS):
+            turn_y(2, 1, r, 4 + r)
+        weave_y(2, 1)
+        for r in range(ROWS):
+            spill_y(2, 0, r)
+        spill_y(2, 1, 0, True)
+        quant_y(2, 1)
+        spill_y(2, 1, 1)
+        spill_y(2, 1, 2, True)
+        spill_y(2, 1, 3)

@@ -22,10 +22,15 @@ PACK = 4
 SPAN = P * PACK
 PASSES = K // SPAN
 GROUPS = A // SPAN
-HALVES = T // SPAN
 ROWS = SPAN // P
 BLOCK = 128
-CUT = ((32, 16, 24, 40), (24, 48, 40, 40), (40, 64, 64, 48))
+BLOCKS = SPAN // BLOCK
+QUADRANTS = 4
+ALL = slice(0, SPAN)
+LOW, HIGH = 0, 4
+
+STRETCHES = SPAN // 8
+V_ALL, V_HALF, V_QUARTER = STRETCHES, STRETCHES // 2, STRETCHES // 4
 
 
 def tile_tanh_policy_action_head_b1_kernel(tc, X_bytes, X_scale, W, bias, half_range, out_0, out_1, out_2):
@@ -36,13 +41,14 @@ def tile_tanh_policy_action_head_b1_kernel(tc, X_bytes, X_scale, W, bias, half_r
         psum = ctx.enter_context(tc.psum_pool(name="psum", bufs=1))
         ctx.enter_context(tc.manual_schedule())
 
-        x_raw, x_sc, w_raw, x_wide, x_in, w_in = {}, {}, {}, {}, {}, {}
-        x_codes, x_scales, w_codes, w_scales = {}, {}, {}, {}
-        acc, y_t, y_in, y_scales, turned = {}, {}, {}, {}, {}
+        x_raw, x_sc, x_wide, x_turned, x_in, x_codes, x_scales = {}, {}, {}, {}, {}, {}, {}
+        w_raw, w_in, w_codes, w_scales = {}, {}, {}, {}
+        acc, y_t, y_turned, y_in, y_words = {}, {}, {}, {}, {}
 
         def load_x_scale(h):
             x_sc[h] = keep.tile([P, ROWS, K // BLOCK], F32, name="x_sc%d" % h)
-            nc.sync.dma_start(out=x_sc[h][:], in_=X_scale[SPAN * h : SPAN * (h + 1), :].rearrange("(r p) j -> p r j", p=P))
+            src = X_scale[SPAN * h : SPAN * (h + 1), :]
+            nc.sync.dma_start(out=x_sc[h][:], in_=src.rearrange("(r p) j -> p r j", p=P))
 
         def load_x(h, c):
             x_raw[h, c] = keep.tile([P, ROWS, SPAN], U8, name="x_raw%d%d" % (h, c))
@@ -54,33 +60,39 @@ def tile_tanh_policy_action_head_b1_kernel(tc, X_bytes, X_scale, W, bias, half_r
             src = W[SPAN * c : SPAN * (c + 1), SPAN * g : SPAN * (g + 1)]
             nc.sync.dma_start(out=w_raw[g, c][:], in_=src.rearrange("(p j) a -> p j a", j=PACK))
 
-        def widen(h, c, r):
-            x_wide[h, c, r] = flow.tile([P, SPAN], BF16, name="x_wide", bufs=8)
-            sorted_view = x_wide[h, c, r][:].rearrange("p (u w e) -> p w u e", u=2, e=2)
-            for q in range(SPAN // BLOCK):
-                j = c * (SPAN // BLOCK) + q
-                nc.vector.tensor_scalar(
-                    out=sorted_view[:, 32 * q : 32 * (q + 1)],
-                    in0=x_raw[h, c][:, r, BLOCK * q : BLOCK * (q + 1)].bitcast(FP8).rearrange("p (w u e) -> p w u e", u=2, e=2),
-                    scalar1=x_sc[h][:, r, j : j + 1],
-                    scalar2=None,
-                    op0=MULT,
-                )
+        def widen(h, c, pair):
+            for r in (2 * pair, 2 * pair + 1):
+                x_wide[h, c, r] = flow.tile([P, SPAN], BF16, name="x_wide", bufs=3 * ROWS)
+                dst = x_wide[h, c, r][:].rearrange("p (u w e) -> p w u e", u=2, e=2)
+                for q in range(BLOCKS):
+                    src = x_raw[h, c][:, r, BLOCK * q : BLOCK * (q + 1)].bitcast(FP8)
+                    j = BLOCKS * c + q
+                    nc.vector.tensor_scalar(
+                        out=dst[:, BLOCK // PACK * q : BLOCK // PACK * (q + 1)],
+                        in0=src.rearrange("p (w u e) -> p w u e", u=2, e=2),
+                        scalar1=x_sc[h][:, r, j : j + 1],
+                        scalar2=None,
+                        op0=MULT,
+                    )
 
-        def turn_x(h, c, b, bank):
-            turned[h, c, b] = psum.tile([P, 2, 2, P], F32, name="bank%d" % bank)
+        def turn_x(h, c, pair, bank):
+            x_turned[h, c, pair] = psum.tile([P, 2, 2, P], F32, name="bank%d" % bank)
             for i in range(2):
-                words = x_wide[h, c, 2 * b + i][:].bitcast(F32)
+                words = x_wide[h, c, 2 * pair + i][:].bitcast(F32)
                 for u in range(2):
-                    nc.tensor.transpose(turned[h, c, b][:, i, u, :], words[:, P * u : P * (u + 1)], ident[:])
+                    nc.tensor.transpose(x_turned[h, c, pair][:, i, u, :], words[:, P * u : P * (u + 1)], ident[:])
 
-        def spill_x(h, c, b):
-            if b == 0:
+        def widen_and_turn(h, c, pair, bank):
+            widen(h, c, pair)
+            turn_x(h, c, pair, bank)
+
+        def spill_x(h, c, pair):
+            if pair == 0:
                 x_in[h, c] = flow.tile([P, SPAN * PACK], BF16, name="x_in", align_bytes=64)
-            dst = x_in[h, c][:].bitcast(F32)[:, 4 * P * b : 4 * P * (b + 1)]
+            dst = x_in[h, c][:].bitcast(F32)[:, SPAN * pair : SPAN * (pair + 1)]
             nc.scalar.copy(
                 out=dst.rearrange("p (i m u) -> p i m u", i=2, u=2),
-                in_=turned[h, c, b][:].rearrange("p i u m -> p i m u"),
+                in_=x_turned[h, c, pair][:].rearrange("p i u m -> p i m u"),
             )
 
         def quant_x(h, c):
@@ -88,98 +100,120 @@ def tile_tanh_policy_action_head_b1_kernel(tc, X_bytes, X_scale, W, bias, half_r
             x_scales[h, c] = keep.tile([P, SPAN], U8, name="x_scales%d%d" % (h, c), align_bytes=64)
             nc.vector.quantize_mx(out=x_codes[h, c][:].bitcast(FP8X4), scales=x_scales[h, c][:], in_=x_in[h, c][:])
 
-        def weave_w(g, c, engine, lo, hi):
-            if lo >= hi:
-                return
+        def weave_w_views(g, c):
             if (g, c) not in w_in:
                 w_in[g, c] = flow.tile([P, SPAN * PACK], BF16, name="w_in", bufs=4, align_bytes=64)
             dst = w_in[g, c][:].rearrange("p (t n i j) -> p n t i j", t=PACK, i=2, j=PACK)
             src = w_raw[g, c][:].rearrange("p j (n i t) -> p n t i j", i=2, t=PACK)
-            if engine == "vector":
-                nc.vector.tensor_copy(out=dst[:, lo:hi], in_=src[:, lo:hi])
-            else:
-                nc.scalar.copy(out=dst[:, lo:hi], in_=src[:, lo:hi])
+            return dst, src
+
+        def weave_w_vector(g, c, share):
+            dst, src = weave_w_views(g, c)
+            nc.vector.tensor_copy(out=dst[:, :share], in_=src[:, :share])
+
+        def weave_w_scalar(g, c, share):
+            dst, src = weave_w_views(g, c)
+            nc.scalar.copy(out=dst[:, share:], in_=src[:, share:])
+
+        def weave_w(g, c, share):
+            weave_w_scalar(g, c, share)
+            weave_w_vector(g, c, share)
 
         def quant_w(g, c):
             w_codes[g, c] = keep.tile([P, SPAN], U32, name="w_codes%d%d" % (g, c), align_bytes=64)
             w_scales[g, c] = keep.tile([P, SPAN], U8, name="w_scales%d%d" % (g, c), align_bytes=64)
             nc.vector.quantize_mx(out=w_codes[g, c][:].bitcast(FP8X4), scales=w_scales[g, c][:], in_=w_in[g, c][:])
 
-        def mm(g, h, t, c, bank):
+        def mm(g, h, t, c, bank, states):
             if c == 0:
                 acc[g, h, t] = psum.tile([P, SPAN], F32, name="bank%d" % bank)
-            cols = slice(P * t, P * (t + 1))
+            slot = slice(P * t, P * (t + 1))
             nc.tensor.matmul_mx(
-                out=acc[g, h, t][:],
-                lhsT=w_codes[g, c][:, cols].bitcast(FP8X4),
-                lhsT_scale=w_scales[g, c][:, cols],
-                rhs=x_codes[h, c][:].bitcast(FP8X4),
-                rhs_scale=x_scales[h, c][:],
+                out=acc[g, h, t][:, states],
+                lhsT=w_codes[g, c][:, slot].bitcast(FP8X4),
+                lhsT_scale=w_scales[g, c][:, slot],
+                rhs=x_codes[h, c][:, states].bitcast(FP8X4),
+                rhs_scale=x_scales[h, c][:, states],
                 start=(c == 0),
                 stop=(c == PASSES - 1),
             )
 
         def mm_pass(g, h, c, bank0, slots=range(PACK)):
             for t in slots:
-                mm(g, h, t, c, bank0 + t)
+                mm(g, h, t, c, bank0 + t, ALL)
 
-        def mm_slot(g, h, t, bank):
+        def mm_slot(g, h, t, bank0, states=ALL):
             for c in range(PASSES):
-                mm(g, h, t, c, bank)
+                mm(g, h, t, c, bank0 + t, states)
 
-        def squash(g, h, t):
+        def squash(g, h, t, states=ALL):
             if (g, h) not in y_t:
                 y_t[g, h] = keep.tile([P, PACK, SPAN], F32, name="y_t%d%d" % (g, h))
             col = PACK * g + t
-            nc.scalar.activation(out=y_t[g, h][:, t, :], in_=acc[g, h, t][:], func=TANH, bias=vecs[:, 0, col : col + 1])
+            nc.scalar.activation(
+                out=y_t[g, h][:, t, states], in_=acc[g, h, t][:, states], func=TANH, bias=vecs[:, 0, col : col + 1]
+            )
 
-        def stretch(g, h, t, on_vector=True):
+        def stretch(g, h, t, states=ALL):
+            col = PACK * g + t
+            row = y_t[g, h][:, t, states]
+            nc.vector.tensor_scalar(out=row, in0=row, scalar1=vecs[:, 1, col : col + 1], scalar2=None, op0=MULT)
+
+        def stretch_on_scalar(g, h, t):
             col = PACK * g + t
             row = y_t[g, h][:, t, :]
-            if on_vector:
-                nc.vector.tensor_scalar(out=row, in0=row, scalar1=vecs[:, 1, col : col + 1], scalar2=None, op0=MULT)
-            else:
-                nc.scalar.activation(out=row, in_=row, func=COPY, scale=vecs[:, 1, col : col + 1])
+            nc.scalar.activation(out=row, in_=row, func=COPY, scale=vecs[:, 1, col : col + 1])
 
         def turn_y(g, h, r, bank):
-            turned[g, h, r, "y"] = psum.tile([P, PACK, P], F32, name="bank%d" % bank)
+            y_turned[g, h, r] = psum.tile([P, PACK, P], F32, name="bank%d" % bank)
             for t in range(PACK):
-                nc.tensor.transpose(turned[g, h, r, "y"][:, t, :], y_t[g, h][:, t, P * r : P * (r + 1)], ident[:])
+                nc.tensor.transpose(y_turned[g, h, r][:, t, :], y_t[g, h][:, t, P * r : P * (r + 1)], ident[:])
 
-        def spill_y(g, h, r, on_vector=False):
-            y_out = flow.tile([P, SPAN], F32, name="y_out", bufs=8)
-            dst = y_out[:].rearrange("p (m t) -> p m t", t=PACK)
-            src = turned[g, h, r, "y"][:].rearrange("p t m -> p m t")
-            if on_vector:
-                nc.vector.tensor_copy(out=dst, in_=src)
-            else:
-                nc.scalar.copy(out=dst, in_=src)
+        def spill_y(g, h, r, copy=nc.scalar.copy):
+            y_out = flow.tile([P, SPAN], F32, name="y_out", bufs=2 * ROWS)
+            copy(
+                out=y_out[:].rearrange("p (m t) -> p m t", t=PACK),
+                in_=y_turned[g, h, r][:].rearrange("p t m -> p m t"),
+            )
             m0 = SPAN * h + P * r
             nc.sync.dma_start(out=out_0[m0 : m0 + P, SPAN * g : SPAN * (g + 1)], in_=y_out[:])
 
-        def weave_y(g, h):
-            y_in[g, h] = flow.tile([P, SPAN * PACK], BF16, name="y_in", bufs=2, align_bytes=64)
+        def weave_y(g, h, states=ALL):
+            width = (states.stop - states.start) * PACK
+            y_in[g, h] = flow.tile([P, width], BF16, name="y_in", bufs=2, align_bytes=64)
             nc.vector.tensor_copy(
                 out=y_in[g, h][:].rearrange("p (n i t) -> p n t i", i=4, t=PACK),
-                in_=y_t[g, h][:].rearrange("p t (n i) -> p n t i", i=4),
+                in_=y_t[g, h][:, :, states].rearrange("p t (n i) -> p n t i", i=4),
             )
 
-        def quant_y(g, h):
-            if h == 0:
-                y_scales[g] = keep.tile([P, T], U8, name="y_scales%d" % g, align_bytes=64)
-            y_words = flow.tile([P, SPAN], U32, name="y_words", align_bytes=64)
-            cols = slice(SPAN * h, SPAN * (h + 1))
-            nc.vector.quantize_mx(out=y_words[:].bitcast(FP8X4), scales=y_scales[g][:, cols], in_=y_in[g, h][:])
-            nc.sync.dma_start(out=out_1[g, :, cols, :].rearrange("p m t -> p (m t)").bitcast(I32), in_=y_words[:].bitcast(I32))
-            if h == HALVES - 1:
-                for q in range(4):
-                    nc.sync.dma_start(out=out_2[g, 4 * q : 4 * q + 4, :].bitcast(I32), in_=y_scales[g][32 * q : 32 * q + 4, :].bitcast(I32))
+        def quant_y(g, h, states=ALL):
+            y_words[g, h] = flow.tile([P, states.stop - states.start], U32, name="y_words", align_bytes=64)
+            scales = y_scales_last[:, 0, :] if g == GROUPS - 1 else y_scales_first[:, g, :]
+            nc.vector.quantize_mx(
+                out=y_words[g, h][:].bitcast(FP8X4),
+                scales=scales[:, SPAN * h + states.start : SPAN * h + states.stop],
+                in_=y_in[g, h][:],
+            )
+
+        def store_words(g, h, states=ALL):
+            dst = out_1[g, :, SPAN * h + states.start : SPAN * h + states.stop, :].rearrange("p m t -> p (m t)")
+            nc.sync.dma_start(out=dst.bitcast(I32), in_=y_words[g, h][:].bitcast(I32))
+
+        def store_scales(scales, groups):
+            for q in range(QUADRANTS):
+                dst = out_2[groups, 4 * q : 4 * q + 4, :].rearrange("g r m -> r g m")
+                nc.sync.dma_start(out=dst.bitcast(I32), in_=scales[32 * q : 32 * q + 4, :, :].bitcast(I32))
+
+        y_scales_first = keep.tile([P, GROUPS - 1, T], U8, name="y_scales_first", align_bytes=64)
+        y_scales_last = keep.tile([P, 1, T], U8, name="y_scales_last", align_bytes=64)
 
         load_x_scale(0)
         load_x(0, 0)
-        for c in range(PASSES):
-            if c + 1 < PASSES:
-                load_x(0, c + 1)
+        load_x(0, 1)
+        load_w(0, 0)
+        load_x(0, 2)
+        load_x(0, 3)
+        for c in range(1, PASSES):
             load_w(0, c)
         vecs_raw = keep.tile([P, 2, 16], BF16, name="vecs_raw")
         for i, vec in enumerate((bias, half_range)):
@@ -197,191 +231,179 @@ def tile_tanh_policy_action_head_b1_kernel(tc, X_bytes, X_scale, W, bias, half_r
 
         ident = keep.tile([P, P], F32, name="ident")
         make_identity(nc, ident[:])
-        warm = keep.tile([P, 1], F32, name="warm")
-        nc.vector.memset(warm[:], 0.0)
-        nc.scalar.activation(out=warm[:], in_=warm[:], func=TANH)
         vecs = keep.tile([P, 2, GROUPS * PACK], F32, name="vecs")
 
-
-        V, S = "vector", "scalar"
-        N = 64
-
-        def x_half(h, c, b, bank0):
-            widen(h, c, 2 * b)
-            widen(h, c, 2 * b + 1)
-            turn_x(h, c, b, bank0 + 2 * (c % 2) + b)
-
-        def wv(g, c):
-            weave_w(g, c, V, 0, CUT[g][c])
-
-        def ws(g, c):
-            weave_w(g, c, S, CUT[g][c], N)
-
-        x_half(0, 0, 0, 4)
-        x_half(0, 0, 1, 4)
-        spill_x(0, 0, 0)
-        spill_x(0, 0, 1)
-        x_half(0, 1, 0, 4)
-        x_half(0, 1, 1, 4)
         for c in range(PASSES):
-            ws(0, c)
-            if c == 3:
-                quant_w(0, 2)
-                mm_pass(0, 0, 2, 0)
-            wv(0, c)
-            quant_x(0, c)
-            if c + 1 < PASSES:
-                spill_x(0, c + 1, 0)
-                spill_x(0, c + 1, 1)
-            if c + 2 < PASSES:
-                x_half(0, c + 2, 0, 4)
-                quant_w(0, c)
-                mm_pass(0, 0, c, 0, (0, 1))
-                x_half(0, c + 2, 1, 4)
-                mm_pass(0, 0, c, 0, (2, 3))
-        ws(1, 0)
-        wv(1, 0)
-        quant_w(0, 3)
-        mm_pass(0, 0, 3, 0)
+            for pair in range(2):
+                widen_and_turn(0, c, pair, HIGH + (2 * c + pair) % 4)
+                if c >= 1:
+                    spill_x(0, c - 1, pair)
+            if c == 2:
+                weave_w_scalar(0, 0, V_HALF)
+            if c >= 2:
+                quant_x(0, c - 2)
+        spill_x(0, 3, 0)
+        spill_x(0, 3, 1)
+        weave_w_vector(0, 0, V_HALF)
+        quant_x(0, 2)
         nc.vector.tensor_copy(out=vecs[:], in_=vecs_raw[:, :, : GROUPS * PACK])
-        def x1(c, b):
-            widen(1, c, 2 * b)
-            widen(1, c, 2 * b + 1)
 
-        wv(1, 1)
-        ws(1, 1)
+        for c in range(PASSES):
+            if c + 1 < PASSES:
+                weave_w(0, c + 1, V_HALF)
+            else:
+                weave_w(1, 0, V_QUARTER)
+            if c == 1:
+                quant_x(0, 3)
+            quant_w(0, c)
+            mm_pass(0, 0, c, LOW)
+
+        weave_w(1, 1, V_HALF)
         quant_w(1, 0)
-        mm_pass(1, 0, 0, 4)
-        wv(1, 2)
-        ws(1, 2)
-        squash(0, 0, 2)
-        squash(0, 0, 3)
+        mm_pass(1, 0, 0, HIGH)
+        for t in range(PACK):
+            squash(0, 0, t)
+        weave_w_vector(1, 2, V_ALL)
         quant_w(1, 1)
-        mm_pass(1, 0, 1, 4)
-        x1(0, 0)
-        turn_x(1, 0, 0, 2)
-        wv(1, 3)
-        ws(1, 3)
-        squash(0, 0, 0)
-        squash(0, 0, 1)
+        mm_pass(1, 0, 1, HIGH)
+        weave_w(1, 3, V_QUARTER)
+        for t in range(PACK):
+            stretch(0, 0, t)
+        for r in range(ROWS):
+            turn_y(0, 0, r, LOW + r)
         quant_w(1, 2)
-        mm_pass(1, 0, 2, 4)
-        x1(0, 1)
-        turn_x(1, 0, 1, 3)
+        mm_pass(1, 0, 2, HIGH)
+        widen(1, 0, 0)
         quant_w(1, 3)
-        mm_pass(1, 0, 3, 4)
+        widen(1, 0, 1)
+        for r in range(ROWS):
+            spill_y(0, 0, r)
+        turn_x(1, 0, 0, LOW)
+        turn_x(1, 0, 1, LOW + 1)
+        mm_pass(1, 0, 3, HIGH)
+
+        widen_and_turn(1, 1, 0, LOW + 2)
+        widen_and_turn(1, 1, 1, LOW + 3)
         spill_x(1, 0, 0)
         spill_x(1, 0, 1)
-        x1(1, 0)
-        turn_x(1, 1, 0, 0)
-        x1(1, 1)
-        turn_x(1, 1, 1, 1)
-        for t in range(PACK):
-            squash(1, 0, t)
+        widen(1, 2, 0)
+        widen(1, 2, 1)
+        squash(1, 0, 0)
+        squash(1, 0, 1)
         quant_x(1, 0)
         spill_x(1, 1, 0)
         spill_x(1, 1, 1)
-        x1(2, 0)
-        turn_x(1, 2, 0, 2)
-        mm_pass(0, 1, 0, 4, (0, 1))
-        x1(2, 1)
-        turn_x(1, 2, 1, 3)
-        mm_pass(0, 1, 0, 4, (2, 3))
-        for t in range(PACK):
-            stretch(0, 0, t)
+        turn_x(1, 2, 0, LOW)
+        turn_x(1, 2, 1, LOW + 1)
+        mm_pass(0, 1, 0, HIGH, (0, 1))
+        squash(1, 0, 2)
+        squash(1, 0, 3)
+        widen_and_turn(1, 3, 0, LOW + 2)
+        mm_pass(0, 1, 0, HIGH, (2, 3))
+        widen_and_turn(1, 3, 1, LOW + 3)
         quant_x(1, 1)
+        mm_pass(0, 1, 1, HIGH)
         spill_x(1, 2, 0)
         spill_x(1, 2, 1)
-        x1(3, 0)
-        turn_x(1, 3, 0, 0)
-        mm_pass(0, 1, 1, 4, (0, 1))
-        x1(3, 1)
-        turn_x(1, 3, 1, 1)
-        mm_pass(0, 1, 1, 4, (2, 3))
-        turn_y(0, 0, 0, 2)
-        turn_y(0, 0, 1, 3)
-        wv(2, 0)
-        ws(2, 0)
-        quant_x(1, 2)
-        mm_pass(0, 1, 2, 4)
-        spill_x(1, 3, 0)
-        spill_x(1, 3, 1)
-        turn_y(0, 0, 2, 0)
-        turn_y(0, 0, 3, 1)
-        wv(2, 1)
-        ws(2, 1)
-        quant_x(1, 3)
-        mm_pass(0, 1, 3, 4)
-        for r in range(ROWS):
-            spill_y(0, 0, r)
-        quant_w(2, 0)
         for t in range(PACK):
             stretch(1, 0, t)
-        for r in range(ROWS):
-            turn_y(1, 0, r, (r + 2) % 4)
-        wv(2, 2)
-        ws(2, 2)
+        turn_y(1, 0, 0, LOW)
+        turn_y(1, 0, 1, LOW + 1)
+        quant_x(1, 2)
+        mm_pass(0, 1, 2, HIGH)
+        spill_x(1, 3, 0)
+        spill_x(1, 3, 1)
+        turn_y(1, 0, 2, LOW + 2)
+        turn_y(1, 0, 3, LOW + 3)
+        weave_w(2, 0, V_HALF)
+        quant_x(1, 3)
+        mm_pass(0, 1, 3, HIGH)
+        spill_y(1, 0, 0)
+        spill_y(1, 0, 1)
+
+        weave_w(2, 1, V_HALF)
+        quant_w(2, 0)
+        weave_w_vector(2, 2, V_ALL)
         quant_w(2, 1)
         for t in range(PACK):
             squash(0, 1, t)
-            mm_slot(1, 1, t, 4 + t)
-        wv(2, 3)
-        ws(2, 3)
+            mm_slot(1, 1, t, HIGH)
+        spill_y(1, 0, 2)
+        spill_y(1, 0, 3)
+        weave_w_vector(2, 3, V_ALL)
         quant_w(2, 2)
         stretch(0, 1, 0)
         quant_w(2, 3)
         for t in range(1, PACK):
             stretch(0, 1, t)
+        for r in range(ROWS):
+            turn_y(0, 1, r, LOW + r)
+
         weave_y(0, 0)
         for t in range(PACK):
             squash(1, 1, t)
-            spill_y(1, 0, t)
-            mm_slot(2, 0, t, 4 + t)
-        for r in range(ROWS):
-            turn_y(0, 1, r, r)
+            mm_slot(2, 0, t, HIGH)
         stretch(1, 1, 0)
         quant_y(0, 0)
-        weave_y(1, 0)
         for t in range(1, PACK):
             stretch(1, 1, t)
-        quant_y(1, 0)
+        weave_y(1, 0)
+        spill_y(0, 1, 0)
+        store_words(0, 0)
+        for r in range(1, ROWS):
+            spill_y(0, 1, r)
+        for r in range(ROWS):
+            turn_y(1, 1, r, LOW + r)
         weave_y(0, 1)
+        quant_y(1, 0)
+        store_words(1, 0)
+
+        front, back = slice(0, SPAN // 2), slice(SPAN // 2, SPAN)
         for t in range(PACK):
             squash(2, 0, t)
-        for r in range(ROWS):
-            spill_y(0, 1, r)
-        mm_slot(2, 1, 0, 4)
-        mm_slot(2, 1, 1, 5)
-        for r in range(ROWS):
-            turn_y(1, 1, r, r)
-        mm_slot(2, 1, 2, 6)
-        mm_slot(2, 1, 3, 7)
-        stretch(2, 0, 0)
-        quant_y(0, 1)
+            mm_slot(2, 1, t, HIGH, front)
+            if t >= 1:
+                stretch_on_scalar(2, 0, t - 1)
         weave_y(1, 1)
-        for t in range(1, PACK):
-            stretch(2, 0, t)
-        quant_y(1, 1)
-        weave_y(2, 0)
-        squash(2, 1, 0)
-        squash(2, 1, 1)
+        quant_y(0, 1)
+        stretch(2, 0, PACK - 1)
+        store_words(0, 1)
         for r in range(ROWS):
             spill_y(1, 1, r)
-            if r in (1, 2):
-                squash(2, 1, r + 1)
+        for t in range(PACK):
+            squash(2, 1, t, front)
         for r in range(ROWS):
-            turn_y(2, 0, r, r)
-        stretch(2, 1, 0)
+            turn_y(2, 0, r, LOW + r)
+        for t in range(PACK):
+            mm_slot(2, 1, t, HIGH, back)
+        weave_y(2, 0)
+        quant_y(1, 1)
+        store_words(1, 1)
+        store_scales(y_scales_first, slice(0, GROUPS - 1))
+        for t in range(PACK):
+            stretch(2, 1, t, front)
         quant_y(2, 0)
-        for t in range(1, PACK):
-            stretch(2, 1, t)
-        for r in range(ROWS):
-            turn_y(2, 1, r, 4 + r)
-        weave_y(2, 1)
-        for r in range(ROWS):
-            spill_y(2, 0, r)
-        spill_y(2, 1, 0, True)
-        quant_y(2, 1)
+        spill_y(2, 0, 0)
+        spill_y(2, 0, 1)
+        store_words(2, 0)
+        spill_y(2, 0, 2)
+        spill_y(2, 0, 3, nc.vector.tensor_copy)
+        turn_y(2, 1, 0, LOW)
+        turn_y(2, 1, 1, LOW + 1)
+        weave_y(2, 1, front)
+        for t in range(PACK):
+            squash(2, 1, t, back)
+            stretch(2, 1, t, back)
+            if t == 0:
+                quant_y(2, 1, front)
+                store_words(2, 1, front)
+        turn_y(2, 1, 2, HIGH)
+        turn_y(2, 1, 3, HIGH + 1)
+        weave_y(2, 1, back)
+        spill_y(2, 1, 0)
         spill_y(2, 1, 1)
-        spill_y(2, 1, 2, True)
-        spill_y(2, 1, 3)
+        quant_y(2, 1, back)
+        spill_y(2, 1, 2)
+        store_words(2, 1, back)
+        spill_y(2, 1, 3, nc.vector.tensor_copy)
+        store_scales(y_scales_last, slice(GROUPS - 1, GROUPS))

@@ -103,8 +103,8 @@ def tile_tanh_policy_action_head_b1_kernel(tc, X_bytes, X_scale, W, bias, half_r
         def weave_w_views(g, c):
             if (g, c) not in w_in:
                 w_in[g, c] = flow.tile([P, SPAN * PACK], BF16, name="w_in", bufs=4, align_bytes=64)
-            dst = w_in[g, c][:].rearrange("p (t n i j) -> p n t i j", t=PACK, i=2, j=PACK)
-            src = w_raw[g, c][:].rearrange("p j (n i t) -> p n t i j", i=2, t=PACK)
+            dst = w_in[g, c][:].rearrange("p (t n i j) -> p n t j i", t=PACK, i=2, j=PACK)
+            src = w_raw[g, c][:].rearrange("p j (n i t) -> p n t j i", i=2, t=PACK)
             return dst, src
 
         def weave_w_vector(g, c, share):

@@ -30,7 +30,7 @@ ALL = slice(0, SPAN)
 LOW, HIGH = 0, 4
 
 STRETCHES = SPAN // 8
-V_ALL, V_HALF, V_QUARTER = STRETCHES, STRETCHES // 2, STRETCHES // 4
+V_ALL, V_MOST, V_HALF, V_QUARTER = STRETCHES, 3 * STRETCHES // 4, STRETCHES // 2, STRETCHES // 4
 
 
 def tile_tanh_policy_action_head_b1_kernel(tc, X_bytes, X_scale, W, bias, half_range, out_0, out_1, out_2):
@@ -50,10 +50,12 @@ def tile_tanh_policy_action_head_b1_kernel(tc, X_bytes, X_scale, W, bias, half_r
             src = X_scale[SPAN * h : SPAN * (h + 1), :]
             nc.sync.dma_start(out=x_sc[h][:], in_=src.rearrange("(r p) j -> p r j", p=P))
 
-        def load_x(h, c):
-            x_raw[h, c] = keep.tile([P, ROWS, SPAN], U8, name="x_raw%d%d" % (h, c))
-            src = X_bytes[SPAN * h : SPAN * (h + 1), SPAN * c : SPAN * (c + 1)]
-            nc.sync.dma_start(out=x_raw[h, c][:], in_=src.rearrange("(r p) k -> p r k", p=P))
+        def load_x(h, c, r0=0, r1=ROWS):
+            raw = keep.tile([P, r1 - r0, SPAN], U8, name="x_raw%d%d%d" % (h, c, r0))
+            src = X_bytes[SPAN * h + P * r0 : SPAN * h + P * r1, SPAN * c : SPAN * (c + 1)]
+            nc.sync.dma_start(out=raw[:], in_=src.rearrange("(r p) k -> p r k", p=P))
+            for r in range(r0, r1):
+                x_raw[h, c, r] = raw[:, r - r0, :]
 
         def load_w(g, c):
             w_raw[g, c] = keep.tile([P, PACK, SPAN], BF16, name="w_raw%d%d" % (g, c))
@@ -65,7 +67,7 @@ def tile_tanh_policy_action_head_b1_kernel(tc, X_bytes, X_scale, W, bias, half_r
                 x_wide[h, c, r] = flow.tile([P, SPAN], BF16, name="x_wide", bufs=3 * ROWS)
                 dst = x_wide[h, c, r][:].rearrange("p (u w e) -> p w u e", u=2, e=2)
                 for q in range(BLOCKS):
-                    src = x_raw[h, c][:, r, BLOCK * q : BLOCK * (q + 1)].bitcast(FP8)
+                    src = x_raw[h, c, r][:, BLOCK * q : BLOCK * (q + 1)].bitcast(FP8)
                     j = BLOCKS * c + q
                     nc.vector.tensor_scalar(
                         out=dst[:, BLOCK // PACK * q : BLOCK // PACK * (q + 1)],
@@ -102,7 +104,7 @@ def tile_tanh_policy_action_head_b1_kernel(tc, X_bytes, X_scale, W, bias, half_r
 
         def weave_w_views(g, c):
             if (g, c) not in w_in:
-                w_in[g, c] = flow.tile([P, SPAN * PACK], BF16, name="w_in", bufs=4, align_bytes=64)
+                w_in[g, c] = flow.tile([P, SPAN * PACK], BF16, name="w_in", align_bytes=64)
             dst = w_in[g, c][:].rearrange("p (t n i j) -> p n t j i", t=PACK, i=2, j=PACK)
             src = w_raw[g, c][:].rearrange("p j (n i t) -> p n t j i", i=2, t=PACK)
             return dst, src
@@ -180,7 +182,7 @@ def tile_tanh_policy_action_head_b1_kernel(tc, X_bytes, X_scale, W, bias, half_r
 
         def weave_y(g, h, states=ALL):
             width = (states.stop - states.start) * PACK
-            y_in[g, h] = flow.tile([P, width], BF16, name="y_in", bufs=2, align_bytes=64)
+            y_in[g, h] = flow.tile([P, width], BF16, name="y_in", align_bytes=64)
             nc.vector.tensor_copy(
                 out=y_in[g, h][:].rearrange("p (n i t) -> p n t i", i=4, t=PACK),
                 in_=y_t[g, h][:, :, states].rearrange("p t (n i) -> p n t i", i=4),
@@ -188,10 +190,9 @@ def tile_tanh_policy_action_head_b1_kernel(tc, X_bytes, X_scale, W, bias, half_r
 
         def quant_y(g, h, states=ALL):
             y_words[g, h] = flow.tile([P, states.stop - states.start], U32, name="y_words", align_bytes=64)
-            scales = y_scales_last[:, 0, :] if g == GROUPS - 1 else y_scales_first[:, g, :]
             nc.vector.quantize_mx(
                 out=y_words[g, h][:].bitcast(FP8X4),
-                scales=scales[:, SPAN * h + states.start : SPAN * h + states.stop],
+                scales=y_scales[:, g, SPAN * h + states.start : SPAN * h + states.stop],
                 in_=y_in[g, h][:],
             )
 
@@ -199,16 +200,16 @@ def tile_tanh_policy_action_head_b1_kernel(tc, X_bytes, X_scale, W, bias, half_r
             dst = out_1[g, :, SPAN * h + states.start : SPAN * h + states.stop, :].rearrange("p m t -> p (m t)")
             nc.sync.dma_start(out=dst.bitcast(I32), in_=y_words[g, h][:].bitcast(I32))
 
-        def store_scales(scales, groups):
+        def store_scales():
             for q in range(QUADRANTS):
-                dst = out_2[groups, 4 * q : 4 * q + 4, :].rearrange("g r m -> r g m")
-                nc.sync.dma_start(out=dst.bitcast(I32), in_=scales[32 * q : 32 * q + 4, :, :].bitcast(I32))
+                dst = out_2[:, 4 * q : 4 * q + 4, :].rearrange("g r m -> r g m")
+                nc.sync.dma_start(out=dst.bitcast(I32), in_=y_scales[32 * q : 32 * q + 4, :, :].bitcast(I32))
 
-        y_scales_first = keep.tile([P, GROUPS - 1, T], U8, name="y_scales_first", align_bytes=64)
-        y_scales_last = keep.tile([P, 1, T], U8, name="y_scales_last", align_bytes=64)
+        y_scales = keep.tile([P, GROUPS, T], U8, name="y_scales", align_bytes=64)
 
         load_x_scale(0)
-        load_x(0, 0)
+        load_x(0, 0, 0, ROWS // 2)
+        load_x(0, 0, ROWS // 2, ROWS)
         load_x(0, 1)
         load_w(0, 0)
         load_x(0, 2)
@@ -233,32 +234,43 @@ def tile_tanh_policy_action_head_b1_kernel(tc, X_bytes, X_scale, W, bias, half_r
         make_identity(nc, ident[:])
         vecs = keep.tile([P, 2, GROUPS * PACK], F32, name="vecs")
 
-        for c in range(PASSES):
+        for c in range(2):
             for pair in range(2):
-                widen_and_turn(0, c, pair, HIGH + (2 * c + pair) % 4)
-                if c >= 1:
-                    spill_x(0, c - 1, pair)
-            if c == 2:
-                weave_w_scalar(0, 0, V_HALF)
-            if c >= 2:
-                quant_x(0, c - 2)
+                widen_and_turn(0, c, pair, HIGH + 2 * c + pair)
+        spill_x(0, 0, 0)
+        weave_w_scalar(0, 0, V_QUARTER)
+        spill_x(0, 0, 1)
+        widen_and_turn(0, 2, 0, LOW)
+        widen_and_turn(0, 2, 1, LOW + 1)
+        spill_x(0, 1, 0)
+        spill_x(0, 1, 1)
+        weave_w_vector(0, 0, V_QUARTER)
+        widen_and_turn(0, 3, 0, HIGH)
+        widen_and_turn(0, 3, 1, HIGH + 1)
+        quant_x(0, 0)
+        spill_x(0, 2, 0)
+        spill_x(0, 2, 1)
+
+        weave_w(0, 1, V_HALF)
+        quant_w(0, 0)
+        mm_pass(0, 0, 0, LOW)
+        weave_w(0, 2, V_HALF)
+        quant_x(0, 1)
+        quant_w(0, 1)
+        mm_pass(0, 0, 1, LOW)
         spill_x(0, 3, 0)
         spill_x(0, 3, 1)
-        weave_w_vector(0, 0, V_HALF)
         quant_x(0, 2)
+        quant_w(0, 2)
+        mm_pass(0, 0, 2, LOW)
+        weave_w(0, 3, V_HALF)
+        weave_w(1, 0, V_QUARTER)
+        quant_x(0, 3)
+        quant_w(0, 3)
+        mm_pass(0, 0, 3, LOW)
         nc.vector.tensor_copy(out=vecs[:], in_=vecs_raw[:, :, : GROUPS * PACK])
 
-        for c in range(PASSES):
-            if c + 1 < PASSES:
-                weave_w(0, c + 1, V_HALF)
-            else:
-                weave_w(1, 0, V_QUARTER)
-            if c == 1:
-                quant_x(0, 3)
-            quant_w(0, c)
-            mm_pass(0, 0, c, LOW)
-
-        weave_w(1, 1, V_HALF)
+        weave_w(1, 1, V_MOST)
         quant_w(1, 0)
         mm_pass(1, 0, 0, HIGH)
         for t in range(PACK):
@@ -266,13 +278,15 @@ def tile_tanh_policy_action_head_b1_kernel(tc, X_bytes, X_scale, W, bias, half_r
         weave_w_vector(1, 2, V_ALL)
         quant_w(1, 1)
         mm_pass(1, 0, 1, HIGH)
-        weave_w(1, 3, V_QUARTER)
-        for t in range(PACK):
-            stretch(0, 0, t)
+        stretch_on_scalar(0, 0, 0)
+        stretch_on_scalar(0, 0, 1)
+        stretch(0, 0, 2)
+        stretch(0, 0, 3)
         for r in range(ROWS):
             turn_y(0, 0, r, LOW + r)
         quant_w(1, 2)
         mm_pass(1, 0, 2, HIGH)
+        weave_w(1, 3, V_HALF)
         widen(1, 0, 0)
         quant_w(1, 3)
         widen(1, 0, 1)
@@ -299,27 +313,23 @@ def tile_tanh_policy_action_head_b1_kernel(tc, X_bytes, X_scale, W, bias, half_r
         squash(1, 0, 2)
         squash(1, 0, 3)
         widen_and_turn(1, 3, 0, LOW + 2)
-        mm_pass(0, 1, 0, HIGH, (2, 3))
         widen_and_turn(1, 3, 1, LOW + 3)
+        mm_pass(0, 1, 0, HIGH, (2, 3))
         quant_x(1, 1)
         mm_pass(0, 1, 1, HIGH)
         spill_x(1, 2, 0)
         spill_x(1, 2, 1)
         for t in range(PACK):
             stretch(1, 0, t)
-        turn_y(1, 0, 0, LOW)
-        turn_y(1, 0, 1, LOW + 1)
-        quant_x(1, 2)
-        mm_pass(0, 1, 2, HIGH)
         spill_x(1, 3, 0)
         spill_x(1, 3, 1)
-        turn_y(1, 0, 2, LOW + 2)
-        turn_y(1, 0, 3, LOW + 3)
+        for r in range(ROWS):
+            turn_y(1, 0, r, LOW + r)
+        quant_x(1, 2)
+        mm_pass(0, 1, 2, HIGH)
         weave_w(2, 0, V_HALF)
         quant_x(1, 3)
         mm_pass(0, 1, 3, HIGH)
-        spill_y(1, 0, 0)
-        spill_y(1, 0, 1)
 
         weave_w(2, 1, V_HALF)
         quant_w(2, 0)
@@ -328,8 +338,8 @@ def tile_tanh_policy_action_head_b1_kernel(tc, X_bytes, X_scale, W, bias, half_r
         for t in range(PACK):
             squash(0, 1, t)
             mm_slot(1, 1, t, HIGH)
-        spill_y(1, 0, 2)
-        spill_y(1, 0, 3)
+        for r in range(ROWS):
+            spill_y(1, 0, r)
         weave_w_vector(2, 3, V_ALL)
         quant_w(2, 2)
         stretch(0, 1, 0)
@@ -379,7 +389,6 @@ def tile_tanh_policy_action_head_b1_kernel(tc, X_bytes, X_scale, W, bias, half_r
         weave_y(2, 0)
         quant_y(1, 1)
         store_words(1, 1)
-        store_scales(y_scales_first, slice(0, GROUPS - 1))
         for t in range(PACK):
             stretch(2, 1, t, front)
         quant_y(2, 0)
@@ -406,4 +415,4 @@ def tile_tanh_policy_action_head_b1_kernel(tc, X_bytes, X_scale, W, bias, half_r
         spill_y(2, 1, 2)
         store_words(2, 1, back)
         spill_y(2, 1, 3, nc.vector.tensor_copy)
-        store_scales(y_scales_last, slice(GROUPS - 1, GROUPS))
+        store_scales()

from contextlib import ExitStack

import concourse.mybir as mybir
from concourse.masks import make_identity

T, K, A = 1024, 2048, 1536
FLOPS = 2 * T * K * A

F32 = mybir.dt.float32
BF16 = mybir.dt.bfloat16
I32 = mybir.dt.int32
U32 = mybir.dt.uint32
U8 = mybir.dt.uint8
FP8 = mybir.dt.float8_e4m3fn
FP8X4 = mybir.dt.float8_e4m3fn_x4
MULT = mybir.AluOpType.mult
COPY = mybir.ActivationFunctionType.Copy
TANH = mybir.ActivationFunctionType.Tanh

P = 128
PACK = 4
SPAN = P * PACK
PASSES = K // SPAN
GROUPS = A // SPAN
ROWS = SPAN // P
BLOCK = 128
BLOCKS = SPAN // BLOCK
QUADRANTS = 4
ALL = slice(0, SPAN)
LOW, HIGH = 0, 4

STRETCHES = SPAN // 8
V_ALL, V_MOST, V_HALF, V_QUARTER = STRETCHES, 3 * STRETCHES // 4, STRETCHES // 2, STRETCHES // 4


def tile_tanh_policy_action_head_b1_kernel(tc, X_bytes, X_scale, W, bias, half_range, out_0, out_1, out_2):
    nc = tc.nc
    with ExitStack() as ctx:
        keep = ctx.enter_context(tc.tile_pool(name="keep", bufs=1))
        flow = ctx.enter_context(tc.tile_pool(name="flow", bufs=3))
        psum = ctx.enter_context(tc.psum_pool(name="psum", bufs=1))
        ctx.enter_context(tc.manual_schedule())

        x_raw, x_sc, x_wide, x_turned, x_in, x_codes, x_scales = {}, {}, {}, {}, {}, {}, {}
        w_raw, w_in, w_codes, w_scales = {}, {}, {}, {}
        acc, y_t, y_turned, y_in, y_words = {}, {}, {}, {}, {}

        def load_x_scale(h):
            x_sc[h] = keep.tile([P, ROWS, K // BLOCK], F32, name="x_sc%d" % h)
            src = X_scale[SPAN * h : SPAN * (h + 1), :]
            nc.sync.dma_start(out=x_sc[h][:], in_=src.rearrange("(r p) j -> p r j", p=P))

        def load_x(h, c, r0=0, r1=ROWS):
            raw = keep.tile([P, r1 - r0, SPAN], U8, name="x_raw%d%d%d" % (h, c, r0))
            src = X_bytes[SPAN * h + P * r0 : SPAN * h + P * r1, SPAN * c : SPAN * (c + 1)]
            nc.sync.dma_start(out=raw[:], in_=src.rearrange("(r p) k -> p r k", p=P))
            for r in range(r0, r1):
                x_raw[h, c, r] = raw[:, r - r0, :]

        def load_w(g, c):
            w_raw[g, c] = keep.tile([P, PACK, SPAN], BF16, name="w_raw%d%d" % (g, c))
            src = W[SPAN * c : SPAN * (c + 1), SPAN * g : SPAN * (g + 1)]
            nc.sync.dma_start(out=w_raw[g, c][:], in_=src.rearrange("(p j) a -> p j a", j=PACK))

        def widen(h, c, pair):
            for r in (2 * pair, 2 * pair + 1):
                x_wide[h, c, r] = flow.tile([P, SPAN], BF16, name="x_wide", bufs=3 * ROWS)
                dst = x_wide[h, c, r][:].rearrange("p (u w e) -> p w u e", u=2, e=2)
                for q in range(BLOCKS):
                    src = x_raw[h, c, r][:, BLOCK * q : BLOCK * (q + 1)].bitcast(FP8)
                    j = BLOCKS * c + q
                    nc.vector.tensor_scalar(
                        out=dst[:, BLOCK // PACK * q : BLOCK // PACK * (q + 1)],
                        in0=src.rearrange("p (w u e) -> p w u e", u=2, e=2),
                        scalar1=x_sc[h][:, r, j : j + 1],
                        scalar2=None,
                        op0=MULT,
                    )

        def turn_x(h, c, pair, bank):
            x_turned[h, c, pair] = psum.tile([P, 2, 2, P], F32, name="bank%d" % bank)
            for i in range(2):
                words = x_wide[h, c, 2 * pair + i][:].bitcast(F32)
                for u in range(2):
                    nc.tensor.transpose(x_turned[h, c, pair][:, i, u, :], words[:, P * u : P * (u + 1)], ident[:])

        def widen_and_turn(h, c, pair, bank):
            widen(h, c, pair)
            turn_x(h, c, pair, bank)

        def spill_x(h, c, pair):
            if pair == 0:
                x_in[h, c] = flow.tile([P, SPAN * PACK], BF16, name="x_in", align_bytes=64)
            dst = x_in[h, c][:].bitcast(F32)[:, SPAN * pair : SPAN * (pair + 1)]
            nc.scalar.copy(
                out=dst.rearrange("p (i m u) -> p i m u", i=2, u=2),
                in_=x_turned[h, c, pair][:].rearrange("p i u m -> p i m u"),
            )

        def quant_x(h, c):
            x_codes[h, c] = keep.tile([P, SPAN], U32, name="x_codes%d%d" % (h, c), align_bytes=64)
            x_scales[h, c] = keep.tile([P, SPAN], U8, name="x_scales%d%d" % (h, c), align_bytes=64)
            nc.vector.quantize_mx(out=x_codes[h, c][:].bitcast(FP8X4), scales=x_scales[h, c][:], in_=x_in[h, c][:])

        def weave_w_views(g, c):
            if (g, c) not in w_in:
                w_in[g, c] = flow.tile([P, SPAN * PACK], BF16, name="w_in", align_bytes=64)
            dst = w_in[g, c][:].rearrange("p (t n i j) -> p n t j i", t=PACK, i=2, j=PACK)
            src = w_raw[g, c][:].rearrange("p j (n i t) -> p n t j i", i=2, t=PACK)
            return dst, src

        def weave_w_vector(g, c, share):
            dst, src = weave_w_views(g, c)
            nc.vector.tensor_copy(out=dst[:, :share], in_=src[:, :share])

        def weave_w_scalar(g, c, share):
            dst, src = weave_w_views(g, c)
            nc.scalar.copy(out=dst[:, share:], in_=src[:, share:])

        def weave_w(g, c, share):
            weave_w_scalar(g, c, share)
            weave_w_vector(g, c, share)

        def quant_w(g, c):
            w_codes[g, c] = keep.tile([P, SPAN], U32, name="w_codes%d%d" % (g, c), align_bytes=64)
            w_scales[g, c] = keep.tile([P, SPAN], U8, name="w_scales%d%d" % (g, c), align_bytes=64)
            nc.vector.quantize_mx(out=w_codes[g, c][:].bitcast(FP8X4), scales=w_scales[g, c][:], in_=w_in[g, c][:])

        def mm(g, h, t, c, bank, states):
            if c == 0:
                acc[g, h, t] = psum.tile([P, SPAN], F32, name="bank%d" % bank)
            slot = slice(P * t, P * (t + 1))
            nc.tensor.matmul_mx(
                out=acc[g, h, t][:, states],
                lhsT=w_codes[g, c][:, slot].bitcast(FP8X4),
                lhsT_scale=w_scales[g, c][:, slot],
                rhs=x_codes[h, c][:, states].bitcast(FP8X4),
                rhs_scale=x_scales[h, c][:, states],
                start=(c == 0),
                stop=(c == PASSES - 1),
            )

        def mm_pass(g, h, c, bank0, slots=range(PACK)):
            for t in slots:
                mm(g, h, t, c, bank0 + t, ALL)

        def mm_slot(g, h, t, bank0, states=ALL):
            for c in range(PASSES):
                mm(g, h, t, c, bank0 + t, states)

        def squash(g, h, t, states=ALL):
            if (g, h) not in y_t:
                y_t[g, h] = keep.tile([P, PACK, SPAN], F32, name="y_t%d%d" % (g, h))
            col = PACK * g + t
            nc.scalar.activation(
                out=y_t[g, h][:, t, states], in_=acc[g, h, t][:, states], func=TANH, bias=vecs[:, 0, col : col + 1]
            )

        def stretch(g, h, t, states=ALL):
            col = PACK * g + t
            row = y_t[g, h][:, t, states]
            nc.vector.tensor_scalar(out=row, in0=row, scalar1=vecs[:, 1, col : col + 1], scalar2=None, op0=MULT)

        def stretch_on_scalar(g, h, t):
            col = PACK * g + t
            row = y_t[g, h][:, t, :]
            nc.scalar.activation(out=row, in_=row, func=COPY, scale=vecs[:, 1, col : col + 1])

        def turn_y(g, h, r, bank):
            y_turned[g, h, r] = psum.tile([P, PACK, P], F32, name="bank%d" % bank)
            for t in range(PACK):
                nc.tensor.transpose(y_turned[g, h, r][:, t, :], y_t[g, h][:, t, P * r : P * (r + 1)], ident[:])

        def spill_y(g, h, r, copy=nc.scalar.copy):
            y_out = flow.tile([P, SPAN], F32, name="y_out", bufs=2 * ROWS)
            copy(
                out=y_out[:].rearrange("p (m t) -> p m t", t=PACK),
                in_=y_turned[g, h, r][:].rearrange("p t m -> p m t"),
            )
            m0 = SPAN * h + P * r
            nc.sync.dma_start(out=out_0[m0 : m0 + P, SPAN * g : SPAN * (g + 1)], in_=y_out[:])

        def weave_y(g, h, states=ALL):
            width = (states.stop - states.start) * PACK
            y_in[g, h] = flow.tile([P, width], BF16, name="y_in", align_bytes=64)
            nc.vector.tensor_copy(
                out=y_in[g, h][:].rearrange("p (n i t) -> p n t i", i=4, t=PACK),
                in_=y_t[g, h][:, :, states].rearrange("p t (n i) -> p n t i", i=4),
            )

        def quant_y(g, h, states=ALL):
            y_words[g, h] = flow.tile([P, states.stop - states.start], U32, name="y_words", align_bytes=64)
            nc.vector.quantize_mx(
                out=y_words[g, h][:].bitcast(FP8X4),
                scales=y_scales[:, g, SPAN * h + states.start : SPAN * h + states.stop],
                in_=y_in[g, h][:],
            )

        def store_words(g, h, states=ALL):
            dst = out_1[g, :, SPAN * h + states.start : SPAN * h + states.stop, :].rearrange("p m t -> p (m t)")
            nc.sync.dma_start(out=dst.bitcast(I32), in_=y_words[g, h][:].bitcast(I32))

        def store_scales():
            for q in range(QUADRANTS):
                dst = out_2[:, 4 * q : 4 * q + 4, :].rearrange("g r m -> r g m")
                nc.sync.dma_start(out=dst.bitcast(I32), in_=y_scales[32 * q : 32 * q + 4, :, :].bitcast(I32))

        y_scales = keep.tile([P, GROUPS, T], U8, name="y_scales", align_bytes=64)

        load_x_scale(0)
        load_x(0, 0, 0, ROWS // 2)
        load_x(0, 0, ROWS // 2, ROWS)
        load_x(0, 1)
        load_w(0, 0)
        load_x(0, 2)
        load_x(0, 3)
        for c in range(1, PASSES):
            load_w(0, c)
        vecs_raw = keep.tile([P, 2, 16], BF16, name="vecs_raw")
        for i, vec in enumerate((bias, half_range)):
            nc.sync.dma_start(
                out=vecs_raw[:, i, : GROUPS * PACK].rearrange("p (g t) -> p g t", t=PACK),
                in_=vec.rearrange("(g p t) -> p g t", p=P, t=PACK),
            )
        load_x_scale(1)
        for c in range(PASSES):
            load_w(1, c)
        for c in range(PASSES):
            load_x(1, c)
        for c in range(PASSES):
            load_w(2, c)

        ident = keep.tile([P, P], F32, name="ident")
        make_identity(nc, ident[:])
        vecs = keep.tile([P, 2, GROUPS * PACK], F32, name="vecs")

        for c in range(2):
            for pair in range(2):
                widen_and_turn(0, c, pair, HIGH + 2 * c + pair)
        spill_x(0, 0, 0)
        weave_w_scalar(0, 0, V_QUARTER)
        spill_x(0, 0, 1)
        widen_and_turn(0, 2, 0, LOW)
        widen_and_turn(0, 2, 1, LOW + 1)
        spill_x(0, 1, 0)
        spill_x(0, 1, 1)
        weave_w_vector(0, 0, V_QUARTER)
        widen_and_turn(0, 3, 0, HIGH)
        widen_and_turn(0, 3, 1, HIGH + 1)
        quant_x(0, 0)
        spill_x(0, 2, 0)
        spill_x(0, 2, 1)

        weave_w(0, 1, V_HALF)
        quant_w(0, 0)
        mm_pass(0, 0, 0, LOW)
        weave_w(0, 2, V_HALF)
        quant_x(0, 1)
        quant_w(0, 1)
        mm_pass(0, 0, 1, LOW)
        spill_x(0, 3, 0)
        spill_x(0, 3, 1)
        quant_x(0, 2)
        quant_w(0, 2)
        mm_pass(0, 0, 2, LOW)
        weave_w(0, 3, V_HALF)
        weave_w(1, 0, V_QUARTER)
        quant_x(0, 3)
        quant_w(0, 3)
        mm_pass(0, 0, 3, LOW)
        nc.vector.tensor_copy(out=vecs[:], in_=vecs_raw[:, :, : GROUPS * PACK])

        weave_w(1, 1, V_MOST)
        quant_w(1, 0)
        mm_pass(1, 0, 0, HIGH)
        for t in range(PACK):
            squash(0, 0, t)
        weave_w_vector(1, 2, V_ALL)
        quant_w(1, 1)
        mm_pass(1, 0, 1, HIGH)
        stretch_on_scalar(0, 0, 0)
        stretch_on_scalar(0, 0, 1)
        stretch(0, 0, 2)
        stretch(0, 0, 3)
        for r in range(ROWS):
            turn_y(0, 0, r, LOW + r)
        quant_w(1, 2)
        mm_pass(1, 0, 2, HIGH)
        weave_w(1, 3, V_HALF)
        widen(1, 0, 0)
        quant_w(1, 3)
        widen(1, 0, 1)
        for r in range(ROWS):
            spill_y(0, 0, r)
        turn_x(1, 0, 0, LOW)
        turn_x(1, 0, 1, LOW + 1)
        mm_pass(1, 0, 3, HIGH)

        widen_and_turn(1, 1, 0, LOW + 2)
        widen_and_turn(1, 1, 1, LOW + 3)
        spill_x(1, 0, 0)
        spill_x(1, 0, 1)
        widen(1, 2, 0)
        widen(1, 2, 1)
        squash(1, 0, 0)
        squash(1, 0, 1)
        quant_x(1, 0)
        spill_x(1, 1, 0)
        spill_x(1, 1, 1)
        turn_x(1, 2, 0, LOW)
        turn_x(1, 2, 1, LOW + 1)
        mm_pass(0, 1, 0, HIGH, (0, 1))
        squash(1, 0, 2)
        squash(1, 0, 3)
        widen_and_turn(1, 3, 0, LOW + 2)
        widen_and_turn(1, 3, 1, LOW + 3)
        mm_pass(0, 1, 0, HIGH, (2, 3))
        quant_x(1, 1)
        mm_pass(0, 1, 1, HIGH)
        spill_x(1, 2, 0)
        spill_x(1, 2, 1)
        for t in range(PACK):
            stretch(1, 0, t)
        spill_x(1, 3, 0)
        spill_x(1, 3, 1)
        for r in range(ROWS):
            turn_y(1, 0, r, LOW + r)
        quant_x(1, 2)
        mm_pass(0, 1, 2, HIGH)
        weave_w(2, 0, V_HALF)
        quant_x(1, 3)
        mm_pass(0, 1, 3, HIGH)

        weave_w(2, 1, V_HALF)
        quant_w(2, 0)
        weave_w_vector(2, 2, V_ALL)
        quant_w(2, 1)
        for t in range(PACK):
            squash(0, 1, t)
            mm_slot(1, 1, t, HIGH)
        for r in range(ROWS):
            spill_y(1, 0, r)
        weave_w_vector(2, 3, V_ALL)
        quant_w(2, 2)
        stretch(0, 1, 0)
        quant_w(2, 3)
        for t in range(1, PACK):
            stretch(0, 1, t)
        for r in range(ROWS):
            turn_y(0, 1, r, LOW + r)

        weave_y(0, 0)
        for t in range(PACK):
            squash(1, 1, t)
            mm_slot(2, 0, t, HIGH)
        stretch(1, 1, 0)
        quant_y(0, 0)
        for t in range(1, PACK):
            stretch(1, 1, t)
        weave_y(1, 0)
        spill_y(0, 1, 0)
        store_words(0, 0)
        for r in range(1, ROWS):
            spill_y(0, 1, r)
        for r in range(ROWS):
            turn_y(1, 1, r, LOW + r)
        weave_y(0, 1)
        quant_y(1, 0)
        store_words(1, 0)

        front, back = slice(0, SPAN // 2), slice(SPAN // 2, SPAN)
        for t in range(PACK):
            squash(2, 0, t)
            mm_slot(2, 1, t, HIGH, front)
            if t >= 1:
                stretch_on_scalar(2, 0, t - 1)
        weave_y(1, 1)
        quant_y(0, 1)
        stretch(2, 0, PACK - 1)
        store_words(0, 1)
        for r in range(ROWS):
            spill_y(1, 1, r)
        for t in range(PACK):
            squash(2, 1, t, front)
        for r in range(ROWS):
            turn_y(2, 0, r, LOW + r)
        for t in range(PACK):
            mm_slot(2, 1, t, HIGH, back)
        weave_y(2, 0)
        quant_y(1, 1)
        store_words(1, 1)
        for t in range(PACK):
            stretch(2, 1, t, front)
        quant_y(2, 0)
        spill_y(2, 0, 0)
        spill_y(2, 0, 1)
        store_words(2, 0)
        spill_y(2, 0, 2)
        spill_y(2, 0, 3, nc.vector.tensor_copy)
        turn_y(2, 1, 0, LOW)
        turn_y(2, 1, 1, LOW + 1)
        weave_y(2, 1, front)
        for t in range(PACK):
            squash(2, 1, t, back)
            stretch(2, 1, t, back)
            if t == 0:
                quant_y(2, 1, front)
                store_words(2, 1, front)
        turn_y(2, 1, 2, HIGH)
        turn_y(2, 1, 3, HIGH + 1)
        weave_y(2, 1, back)
        spill_y(2, 1, 0)
        spill_y(2, 1, 1)
        quant_y(2, 1, back)
        spill_y(2, 1, 2)
        store_words(2, 1, back)
        spill_y(2, 1, 3, nc.vector.tensor_copy)
        store_scales()
